import numpy as np
import ml_dtypes


def mxq(x, axis, fmt="e4m3"):
    dtype, down = {"e4m3": (ml_dtypes.float8_e4m3fn, 7), "e5m2": (ml_dtypes.float8_e5m2, 14)}[fmt]
    v = np.moveaxis(np.asarray(x, np.float32).astype(ml_dtypes.bfloat16).astype(np.float64), axis, -1)
    blocks = v.reshape(v.shape[:-1] + (-1, 32))
    amax = np.abs(blocks).max(-1, keepdims=True)
    byte = np.maximum(np.where(amax > 0, np.frexp(amax)[1] - 1 + 127, 0) - down, 1)
    scale = np.exp2(byte - 127.0)
    codes = (blocks / scale).astype(np.float32).astype(dtype).astype(np.float64)
    return np.moveaxis((codes * scale).reshape(v.shape), -1, axis)


WIDE = False


def mx_kscale(k):
    if not WIDE:
        return np.ones(k)
    levels = np.array([10, -10, 5, -5, 0])
    if k % 512:
        return np.exp2(np.random.permutation(np.resize(levels, k // 32))).repeat(32)
    a = np.empty((k // 512, 16))
    for p in range(k // 512):
        a[p, :8] = np.random.permutation(np.resize(levels, 8))
        for g in range(8):
            far = levels[np.abs(levels - a[p, g]) >= 10]
            a[p, g + 8] = far[np.random.randint(len(far))]
    return np.exp2(a.ravel()).repeat(32)


def f64(x):
    return np.asarray(x).astype(np.float64)


def striped(idx):
    return np.tile(idx.reshape(-1, 16).T, (8, 1)).astype(np.uint16)


def unstriped(offs):
    return offs[:16].T.reshape(-1).astype(np.int64)


def striped8(idx):
    return np.concatenate([x.reshape(-1, 16).T for x in idx]).astype(np.uint16)


def runs(offs, k):
    lists = np.stack([offs[16 * r : 16 * r + 16].T.reshape(-1) for r in range(8)]).astype(np.int64)
    return lists[np.arange(k) % 512 // 64]


def pack_weight(w):
    k, n = w.shape
    w = f64(np.asarray(w, np.float32).astype(ml_dtypes.bfloat16)).reshape(k // 32, 32, n)
    amax = np.abs(w).max(1)
    byte = np.clip(np.where(amax > 0, np.frexp(amax)[1] - 1 + 127 - 7, 1), 1, 254)
    scaled = (w * np.exp2(127.0 - byte)[:, None, :]).reshape(k, n).astype(np.float32)
    words = np.ascontiguousarray(scaled.reshape(k // 512, 128, 4, n).transpose(0, 1, 3, 2)).astype(ml_dtypes.float8_e4m3fn).view(np.uint8)
    return words, np.ascontiguousarray(byte.astype(np.uint8).reshape(k // 512, 16, n))


def unpack_weight(words, scales):
    g, p, n, _ = words.shape
    vals = np.ascontiguousarray(words).view(ml_dtypes.float8_e4m3fn).astype(np.float64) * np.repeat(np.exp2(scales.astype(np.float64) - 127.0), 8, axis=1)[..., None]
    return vals.transpose(0, 1, 3, 2).reshape(g * 512, n)


E2M1 = np.array([0.0, 0.5, 1.0, 1.5, 2.0, 3.0, 4.0, 6.0, -0.0, -0.5, -1.0, -1.5, -2.0, -3.0, -4.0, -6.0])


def pack_fp4(w):
    k, n = w.shape
    w = f64(np.asarray(w, np.float32).astype(ml_dtypes.bfloat16)).reshape(k // 32, 32, n)
    amax = np.abs(w).max(1)
    mant, ex = np.frexp(amax / 6.0)
    byte = np.clip(np.where(amax > 0, np.where(mant > 0.5, ex, ex - 1) + 127, 1), 1, 254)
    scaled = (w * np.exp2(127.0 - byte)[:, None, :]).reshape(k, n).astype(np.float32)
    c = np.ascontiguousarray(scaled.reshape(k // 512, 128, 4, n).transpose(0, 1, 3, 2)).astype(ml_dtypes.float4_e2m1fn).view(np.uint8) & 0xF
    words = (c[..., 0::2] | (c[..., 1::2] << 4)).reshape(k // 512, 128, 2 * n)
    return np.ascontiguousarray(words), np.ascontiguousarray(byte.astype(np.uint8).reshape(k // 512, 16, n))


def unpack_fp4(words, scales):
    g, _, n = scales.shape
    words = np.ascontiguousarray(words).reshape(g, 128, n, 2)
    nib = np.empty((g, 128, n, 4), np.uint8)
    nib[..., 0::2] = words & 0xF
    nib[..., 1::2] = words >> 4
    vals = E2M1[nib] * np.repeat(np.exp2(scales.astype(np.float64) - 127.0), 8, axis=1)[..., None]
    return vals.transpose(0, 1, 3, 2).reshape(g * 512, n)


def sigmoid(v):
    return 1.0 / (1.0 + np.exp(-np.maximum(v, -700.0)))

def planes(y):
    n, m = y.shape
    v = y.astype(np.float32).astype(ml_dtypes.bfloat16).astype(np.float64).reshape(n // 32, 32, m)
    top = np.abs(v).max(1)
    byte = np.clip(np.where(top > 0, np.frexp(top)[1] - 1 + 127 - 7, 1), 1, 254)
    codes = (v * np.exp2(127.0 - byte)[:, None, :]).reshape(n, m).astype(np.float32).astype(ml_dtypes.float8_e4m3fn).view(np.uint8)
    words = codes.reshape(n // 512, 128, 4, m).transpose(0, 1, 3, 2)
    return np.ascontiguousarray(words), np.ascontiguousarray(byte.astype(np.uint8).reshape(n // 512, 16, m))


K, T, S, V, H, C, J = 512, 2048, 1024, 512, 512, 512, 512


def setup_inputs():
    n = np.random.standard_normal
    s = mx_kscale(K)[:, None]
    packed_xT = pack_weight(n((K, T)) * s)
    packed_w1 = pack_fp4(n((K, H)) / np.sqrt(K) / s)
    return {
        "x_words": packed_xT[0],
        "x_scales": packed_xT[1],
        "w1_words": packed_w1[0],
        "w1_scales": packed_w1[1],
        "gs": (np.random.uniform(0.5, 1.5, (K, 1)) / s).astype(np.float32),
        "tab": n((C, J)).astype(np.float32),
        "offs": striped(np.random.permutation(T)[:S]),
        "n1": striped8(np.stack([np.random.permutation(S) for _ in range(8)])),
        "cand": striped(np.random.permutation(T)[:C]),
        "n2": striped8(np.random.randint(0, J, (8, V))),
        "n3": striped8(np.stack([np.random.permutation(V) for _ in range(8)])),
    }


def reference(x_words, x_scales, w1_words, w1_scales, gs, tab, offs, n1, cand, n2, n3):
    x_cand = unpack_weight(x_words, x_scales)[:, unstriped(cand)]
    xq = unpack_weight(x_words, x_scales)[:, unstriped(offs)]
    y = unpack_fp4(w1_words, w1_scales).T @ xq
    ln = y[np.arange(H)[:, None], runs(n1, H)]
    mx = ln.reshape(H, V, 2).max(axis=2)
    mn = ln.reshape(H, V, 2).min(axis=2)
    z = f64(gs) * (mx * sigmoid(mn))
    s = 0.0625 * ((x_cand.T @ mxq(z, 0, "e4m3")))
    out_0 = np.maximum(s + f64(tab)[np.arange(C)[:, None], runs(n2, C)], s[np.arange(C)[:, None], runs(n3, C)])
    return (out_0,) + planes(out_0)

@@ -1,0 +1,188 @@
+from contextlib import ExitStack
+
+import concourse.mybir as mybir
+
+F32 = mybir.dt.float32
+BF16 = mybir.dt.bfloat16
+I32 = mybir.dt.int32
+U32 = mybir.dt.uint32
+U16 = mybir.dt.uint16
+U8 = mybir.dt.uint8
+FP8X4 = mybir.dt.float8_e4m3fn_x4
+FP4X4 = mybir.dt.float4_e2m1fn_x4
+ALU = mybir.AluOpType
+ACT = mybir.ActivationFunctionType
+
+P = 128
+PACK = 4
+K, T, S, V, H, C, J = 512, 2048, 1024, 512, 512, 512, 512
+BANK = 512
+LANES = 16
+FLOPS = 2 * K * H * S + 2 * K * C * V
+
+Z_CHUNKS = ((0, 256), (256, 512))
+OUT_CHUNKS = ((0, 256), (256, 384), (384, 512))
+
+
+def load_scale_rows(queue, tile, rows):
+    for q in range(4):
+        queue.dma_start(out=tile[32 * q : 32 * q + 4, :].bitcast(I32), in_=rows[4 * q : 4 * q + 4, :].bitcast(I32))
+
+
+def tile_picked_candpgatekind_none_po_kernel(
+    tc, x_words, x_scales, w1_words, w1_scales, gs, tab, offs, n1, cand, n2, n3, out_0, out_1, out_2
+):
+    nc = tc.nc
+    with ExitStack() as ctx:
+        keep = ctx.enter_context(tc.tile_pool(name="keep", bufs=1))
+        ring = ctx.enter_context(tc.tile_pool(name="ring", bufs=2))
+        psum = ctx.enter_context(tc.psum_pool(name="psum", bufs=8))
+
+        offs_t = keep.tile([P, S // LANES], U16, name="offs_t")
+        cand_t = keep.tile([P, C // LANES], U16, name="cand_t")
+        n1_t = keep.tile([P, S // LANES], U16, name="n1_t")
+        n2_t = keep.tile([P, V // LANES], U16, name="n2_t")
+        n3_t = keep.tile([P, V // LANES], U16, name="n3_t")
+        x_w = keep.tile([P, T], U32, name="x_w", align_bytes=64)
+        x_s = keep.tile([P, T], U8, name="x_s", align_bytes=64)
+        w_raw = keep.tile([P, 2 * H], U8, name="w_raw", align_bytes=64)
+        ws_raw = keep.tile([P, H], U8, name="ws_raw", align_bytes=64)
+        gs_t = keep.tile([P, PACK], F32, name="gs_t")
+        tab_t = [keep.tile([P, J], F32, name=f"tab{t}") for t in range(PACK)]
+
+        nc.vector.memset(x_s[:].bitcast(I32), 0)
+        nc.vector.memset(ws_raw[:].bitcast(I32), 0)
+
+        nc.sync.dma_start(out=w_raw[:].bitcast(I32), in_=w1_words[0].bitcast(I32))
+        nc.sync.dma_start(offs_t[:], offs)
+        nc.sync.dma_start(cand_t[:], cand)
+        nc.sync.dma_start(n1_t[:], n1)
+        load_scale_rows(nc.sync, x_s, x_scales[0])
+        load_scale_rows(nc.sync, ws_raw, w1_scales[0])
+        nc.sync.dma_start(out=gs_t[:], in_=gs.rearrange("(p t) o -> p (t o)", t=PACK))
+        nc.sync.dma_start(n2_t[:], n2)
+        nc.sync.dma_start(n3_t[:], n3)
+        nc.sync.dma_start(out=x_w[:].bitcast(I32), in_=x_words[0].rearrange("p c r -> p (c r)").bitcast(I32))
+        tab_rows = tab.rearrange("(p t) j -> p t j", t=PACK)
+        for t in range(PACK):
+            nc.sync.dma_start(out=tab_t[t][:], in_=tab_rows[:, t, :])
+
+        xq_s = keep.tile([P, S], U8, name="xq_s", align_bytes=64)
+        nc.vector.tensor_copy(xq_s[:], x_s[:].indirect(offs_t[:]))
+
+        w_d = keep.tile([P, 2 * H], U8, name="w_d", align_bytes=64)
+        ws_d = keep.tile([P, H], U8, name="ws_d", align_bytes=64)
+        nc.vector.tensor_copy(
+            out=w_d[:].rearrange("p (t m b) -> p t m b", t=PACK, b=2),
+            in_=w_raw[:].rearrange("p (m t b) -> p t m b", t=PACK, b=2),
+        )
+        nc.vector.tensor_copy(
+            out=ws_d[:].rearrange("p (t m) -> p t m", t=PACK),
+            in_=ws_raw[:].rearrange("p (m t) -> p t m", t=PACK),
+        )
+
+        y_t = [keep.tile([P, S], F32, name=f"y{t}") for t in range(PACK)]
+        for h in range(S // BANK):
+            xq_w = ring.tile([P, BANK], U32, name="picked", align_bytes=64)
+            cols = slice(h * BANK, (h + 1) * BANK)
+            nc.vector.tensor_copy(xq_w[:], x_w[:].indirect(offs_t[:, h * BANK // LANES : (h + 1) * BANK // LANES]))
+            for t in range(PACK):
+                acc = psum.tile([P, BANK], F32, name="acc")
+                nc.tensor.matmul_mx(
+                    out=acc[:],
+                    lhsT=w_d[:, 2 * P * t : 2 * P * (t + 1)].bitcast(FP4X4),
+                    lhsT_scale=ws_d[:, P * t : P * (t + 1)],
+                    rhs=xq_w[:].bitcast(FP8X4),
+                    rhs_scale=xq_s[:, cols],
+                    start=True,
+                    stop=True,
+                )
+                nc.scalar.copy(out=y_t[t][:, cols], in_=acc[:])
+
+        xc_s = keep.tile([P, C], U8, name="xc_s", align_bytes=64)
+        xc_w = ring.tile([P, C], U32, name="picked", align_bytes=64)
+        xd_s = keep.tile([P, C], U8, name="xd_s", align_bytes=64)
+        xd_w = keep.tile([P, C], U32, name="xd_w", align_bytes=64)
+        nc.vector.tensor_copy(xc_s[:], x_s[:].indirect(cand_t[:]))
+        nc.vector.tensor_copy(xc_w[:], x_w[:].indirect(cand_t[:]))
+        nc.vector.tensor_copy(
+            out=xd_s[:].rearrange("p (t m) -> p t m", t=PACK),
+            in_=xc_s[:].rearrange("p (m t) -> p t m", t=PACK),
+        )
+        nc.vector.tensor_copy(
+            out=xd_w[:].bitcast(I32).rearrange("p (t m) -> p t m", t=PACK),
+            in_=xc_w[:].bitcast(I32).rearrange("p (m t) -> p t m", t=PACK),
+        )
+
+        s_t = [keep.tile([P, V], F32, name=f"s{t}") for t in range(PACK)]
+        u_all = keep.tile([P, PACK, V], F32, name="u_all")
+        for v0, v1 in Z_CHUNKS:
+            n = v1 - v0
+            ln = keep.tile([P, PACK, 2 * n], F32, name=f"ln{v0}")
+            for t in range(PACK):
+                nc.vector.tensor_copy(ln[:, t, :], y_t[t][:].indirect(n1_t[:, 2 * v0 // LANES : 2 * v1 // LANES]))
+            pairs = ln[:].rearrange("p t (v e) -> p (t v) e", e=2)
+            mn = keep.tile([P, PACK * n], F32, name=f"mn{v0}")
+            mx = keep.tile([P, PACK * n], F32, name=f"mx{v0}")
+            sg = keep.tile([P, PACK * n], F32, name=f"sg{v0}")
+            nc.vector.tensor_tensor(mn[:], pairs[:, :, 0], pairs[:, :, 1], ALU.min)
+            nc.vector.tensor_tensor(mx[:], pairs[:, :, 0], pairs[:, :, 1], ALU.max)
+            nc.scalar.activation(sg[:], mn[:], ACT.Sigmoid)
+            z_rows = keep.tile([P, PACK * n], BF16, name=f"z_rows{v0}")
+            for t in range(PACK):
+                part = slice(t * n, (t + 1) * n)
+                nc.vector.scalar_tensor_tensor(
+                    z_rows[:, part], mx[:, part], gs_t[:, t : t + 1], sg[:, part], ALU.mult, ALU.mult
+                )
+            z_il = keep.tile([P, PACK * n], BF16, name=f"z_il{v0}", align_bytes=64)
+            nc.scalar.copy(
+                out=z_il[:].rearrange("p (c i t) -> p c t i", i=4, t=PACK),
+                in_=z_rows[:].rearrange("p (t c i) -> p c t i", i=4, t=PACK),
+            )
+            z_w = keep.tile([P, n], U32, name=f"z_w{v0}", align_bytes=64)
+            z_s = keep.tile([P, n], U8, name=f"z_s{v0}", align_bytes=64)
+            nc.vector.quantize_mx(out=z_w[:].bitcast(FP8X4), scales=z_s[:], in_=z_il[:])
+            for t in range(PACK):
+                acc = psum.tile([P, BANK], F32, name="acc")
+                nc.tensor.matmul_mx(
+                    out=acc[:, :n],
+                    lhsT=xd_w[:, P * t : P * (t + 1)].bitcast(FP8X4),
+                    lhsT_scale=xd_s[:, P * t : P * (t + 1)],
+                    rhs=z_w[:].bitcast(FP8X4),
+                    rhs_scale=z_s[:],
+                    start=True,
+                    stop=True,
+                )
+                nc.scalar.activation(s_t[t][:, v0:v1], acc[:, :n], ACT.Copy, scale=0.0625)
+            for t in range(PACK):
+                nc.vector.tensor_tensor(
+                    u_all[:, t, v0:v1],
+                    tab_t[t][:].indirect(n2_t[:, v0 // LANES : v1 // LANES]),
+                    s_t[t][:, v0:v1],
+                    ALU.add,
+                )
+
+        out_rows = out_0.rearrange("(p t) v -> p t v", t=PACK)
+        out_words = out_1[0].rearrange("p c r -> p (c r)").bitcast(I32)
+        o_s = keep.tile([P, V], U8, name="o_s", align_bytes=64)
+        for v0, v1 in OUT_CHUNKS:
+            n = v1 - v0
+            paired = keep.tile([P, PACK, n], F32, name=f"paired{v0}")
+            for t in range(PACK):
+                nc.vector.tensor_copy(paired[:, t, :], s_t[t][:].indirect(n3_t[:, v0 // LANES : v1 // LANES]))
+            o = keep.tile([P, PACK, n], F32, name=f"o{v0}")
+            nc.vector.tensor_tensor(o[:], u_all[:, :, v0:v1], paired[:], ALU.max)
+            nc.sync.dma_start(out=out_rows[:, :, v0:v1], in_=o[:])
+            o_il = keep.tile([P, PACK * n], BF16, name=f"o_il{v0}", align_bytes=64)
+            dst = o_il[:].rearrange("p (c i t) -> p c t i", i=4, t=PACK)
+            src = o[:].rearrange("p t (c i) -> p c t i", i=4)
+            if v1 == V:
+                nc.vector.tensor_copy(out=dst, in_=src)
+            else:
+                nc.scalar.copy(out=dst, in_=src)
+            o_w = keep.tile([P, n], U32, name=f"o_w{v0}", align_bytes=64)
+            nc.vector.quantize_mx(out=o_w[:].bitcast(FP8X4), scales=o_s[:, v0:v1], in_=o_il[:])
+            nc.sync.dma_start(out=out_words[:, v0:v1], in_=o_w[:].bitcast(I32))
+        for q in range(4):
+            queue = nc.scalar if q % 2 else nc.sync
+            queue.dma_start(out=out_2[0, 4 * q : 4 * q + 4, :].bitcast(I32), in_=o_s[32 * q : 32 * q + 4, :].bitcast(I32))

@@ -20,8 +20,7 @@ BANK = 512
 LANES = 16
 FLOPS = 2 * K * H * S + 2 * K * C * V
 
-Z_CHUNKS = ((0, 256), (256, 512))
-OUT_CHUNKS = ((0, 256), (256, 384), (384, 512))
+HALF = 256
 
 
 def load_scale_rows(queue, tile, rows):
@@ -35,7 +34,6 @@ def tile_picked_candpgatekind_none_po_kernel(
     nc = tc.nc
     with ExitStack() as ctx:
         keep = ctx.enter_context(tc.tile_pool(name="keep", bufs=1))
-        ring = ctx.enter_context(tc.tile_pool(name="ring", bufs=2))
         psum = ctx.enter_context(tc.psum_pool(name="psum", bufs=8))
 
         offs_t = keep.tile([P, S // LANES], U16, name="offs_t")
@@ -51,18 +49,18 @@ def tile_picked_candpgatekind_none_po_kernel(
         tab_t = [keep.tile([P, J], F32, name=f"tab{t}") for t in range(PACK)]
 
         nc.vector.memset(x_s[:].bitcast(I32), 0)
-        nc.vector.memset(ws_raw[:].bitcast(I32), 0)
+        nc.gpsimd.memset(ws_raw[:].bitcast(I32), 0)
 
         nc.sync.dma_start(out=w_raw[:].bitcast(I32), in_=w1_words[0].bitcast(I32))
         nc.sync.dma_start(offs_t[:], offs)
-        nc.sync.dma_start(cand_t[:], cand)
-        nc.sync.dma_start(n1_t[:], n1)
         load_scale_rows(nc.sync, x_s, x_scales[0])
+        nc.sync.dma_start(out=x_w[:].bitcast(I32), in_=x_words[0].rearrange("p c r -> p (c r)").bitcast(I32))
+        nc.sync.dma_start(cand_t[:], cand)
         load_scale_rows(nc.sync, ws_raw, w1_scales[0])
+        nc.sync.dma_start(n1_t[:], n1)
         nc.sync.dma_start(out=gs_t[:], in_=gs.rearrange("(p t) o -> p (t o)", t=PACK))
         nc.sync.dma_start(n2_t[:], n2)
         nc.sync.dma_start(n3_t[:], n3)
-        nc.sync.dma_start(out=x_w[:].bitcast(I32), in_=x_words[0].rearrange("p c r -> p (c r)").bitcast(I32))
         tab_rows = tab.rearrange("(p t) j -> p t j", t=PACK)
         for t in range(PACK):
             nc.sync.dma_start(out=tab_t[t][:], in_=tab_rows[:, t, :])
@@ -76,31 +74,33 @@ def tile_picked_candpgatekind_none_po_kernel(
             out=w_d[:].rearrange("p (t m b) -> p t m b", t=PACK, b=2),
             in_=w_raw[:].rearrange("p (m t b) -> p t m b", t=PACK, b=2),
         )
-        nc.vector.tensor_copy(
+        nc.gpsimd.tensor_copy(
             out=ws_d[:].rearrange("p (t m) -> p t m", t=PACK),
             in_=ws_raw[:].rearrange("p (m t) -> p t m", t=PACK),
         )
 
-        y_t = [keep.tile([P, S], F32, name=f"y{t}") for t in range(PACK)]
+        xq_w = [keep.tile([P, BANK], U32, name=f"xq_w{h}", align_bytes=64) for h in range(S // BANK)]
         for h in range(S // BANK):
-            xq_w = ring.tile([P, BANK], U32, name="picked", align_bytes=64)
-            cols = slice(h * BANK, (h + 1) * BANK)
-            nc.vector.tensor_copy(xq_w[:], x_w[:].indirect(offs_t[:, h * BANK // LANES : (h + 1) * BANK // LANES]))
-            for t in range(PACK):
-                acc = psum.tile([P, BANK], F32, name="acc")
-                nc.tensor.matmul_mx(
-                    out=acc[:],
-                    lhsT=w_d[:, 2 * P * t : 2 * P * (t + 1)].bitcast(FP4X4),
-                    lhsT_scale=ws_d[:, P * t : P * (t + 1)],
-                    rhs=xq_w[:].bitcast(FP8X4),
-                    rhs_scale=xq_s[:, cols],
-                    start=True,
-                    stop=True,
-                )
-                nc.scalar.copy(out=y_t[t][:, cols], in_=acc[:])
+            nc.vector.tensor_copy(xq_w[h][:], x_w[:].indirect(offs_t[:, h * BANK // LANES : (h + 1) * BANK // LANES]))
+        y_t = [keep.tile([P, S], F32, name=f"y{t}") for t in range(PACK)]
+        for g in range(2):
+            for h in range(S // BANK):
+                cols = slice(h * BANK, (h + 1) * BANK)
+                for t in (2 * g, 2 * g + 1):
+                    acc = psum.tile([P, BANK], F32, name="acc")
+                    nc.tensor.matmul_mx(
+                        out=acc[:],
+                        lhsT=w_d[:, 2 * P * t : 2 * P * (t + 1)].bitcast(FP4X4),
+                        lhsT_scale=ws_d[:, P * t : P * (t + 1)],
+                        rhs=xq_w[h][:].bitcast(FP8X4),
+                        rhs_scale=xq_s[:, cols],
+                        start=True,
+                        stop=True,
+                    )
+                    nc.scalar.copy(out=y_t[t][:, cols], in_=acc[:])
 
         xc_s = keep.tile([P, C], U8, name="xc_s", align_bytes=64)
-        xc_w = ring.tile([P, C], U32, name="picked", align_bytes=64)
+        xc_w = keep.tile([P, C], U32, name="xc_w", align_bytes=64)
         xd_s = keep.tile([P, C], U8, name="xd_s", align_bytes=64)
         xd_w = keep.tile([P, C], U32, name="xd_w", align_bytes=64)
         nc.vector.tensor_copy(xc_s[:], x_s[:].indirect(cand_t[:]))
@@ -115,37 +115,56 @@ def tile_picked_candpgatekind_none_po_kernel(
         )
 
         s_t = [keep.tile([P, V], F32, name=f"s{t}") for t in range(PACK)]
-        u_all = keep.tile([P, PACK, V], F32, name="u_all")
-        for v0, v1 in Z_CHUNKS:
-            n = v1 - v0
-            ln = keep.tile([P, PACK, 2 * n], F32, name=f"ln{v0}")
+        for h in range(V // HALF):
+            v0, v1 = h * HALF, (h + 1) * HALF
+            ln = [keep.tile([P, 2, 2 * HALF], F32, name=f"ln{(g + h) % 2}", align_bytes=64) for g in range(2)]
             for t in range(PACK):
-                nc.vector.tensor_copy(ln[:, t, :], y_t[t][:].indirect(n1_t[:, 2 * v0 // LANES : 2 * v1 // LANES]))
-            pairs = ln[:].rearrange("p t (v e) -> p (t v) e", e=2)
-            mn = keep.tile([P, PACK * n], F32, name=f"mn{v0}")
-            mx = keep.tile([P, PACK * n], F32, name=f"mx{v0}")
-            sg = keep.tile([P, PACK * n], F32, name=f"sg{v0}")
-            nc.vector.tensor_tensor(mn[:], pairs[:, :, 0], pairs[:, :, 1], ALU.min)
-            nc.vector.tensor_tensor(mx[:], pairs[:, :, 0], pairs[:, :, 1], ALU.max)
-            nc.scalar.activation(sg[:], mn[:], ACT.Sigmoid)
-            z_rows = keep.tile([P, PACK * n], BF16, name=f"z_rows{v0}")
-            for t in range(PACK):
-                part = slice(t * n, (t + 1) * n)
-                nc.vector.scalar_tensor_tensor(
-                    z_rows[:, part], mx[:, part], gs_t[:, t : t + 1], sg[:, part], ALU.mult, ALU.mult
+                nc.vector.tensor_copy(
+                    ln[t // 2][:, t % 2, :], y_t[t][:].indirect(n1_t[:, 2 * v0 // LANES : 2 * v1 // LANES])
                 )
-            z_il = keep.tile([P, PACK * n], BF16, name=f"z_il{v0}", align_bytes=64)
+            pairs = [ln[g][:].rearrange("p t (v e) -> p (t v) e", e=2) for g in range(2)]
+            mn = [keep.tile([P, 2 * HALF], F32, name=f"mn{h}_{g}") for g in range(2)]
+            mx_tags = (("mx0_0", "mx0_1"), ("z_il0", "mx1_1"))[h]
+            mx = [keep.tile([P, 2 * HALF], F32, name=mx_tags[g], align_bytes=64) for g in range(2)]
+            sg = [keep.tile([P, 2 * HALF], F32, name=f"sg{h}_{g}") for g in range(2)]
+            for g in range(2):
+                nc.vector.tensor_tensor(mn[g][:], pairs[g][:, :, 0], pairs[g][:, :, 1], ALU.min)
+                nc.scalar.activation(sg[g][:], mn[g][:], ACT.Sigmoid)
+            for g in range(2):
+                nc.vector.tensor_tensor(mx[g][:], pairs[g][:, :, 0], pairs[g][:, :, 1], ALU.max)
+            z_rows = keep.tile([P, PACK * HALF], BF16, name=f"z_rows{h}", align_bytes=64)
+            if h == 0:
+                for g in range(2):
+                    weighted = keep.tile([P, 2 * HALF], F32, name=f"weighted{g}")
+                    for t in (2 * g, 2 * g + 1):
+                        part = slice(t % 2 * HALF, (t % 2 + 1) * HALF)
+                        nc.scalar.activation(weighted[:, part], mx[g][:, part], ACT.Copy, scale=gs_t[:, t : t + 1])
+                    nc.gpsimd.tensor_tensor(
+                        z_rows[:, 2 * g * HALF : 2 * (g + 1) * HALF], weighted[:], sg[g][:], ALU.mult
+                    )
+            else:
+                for t in range(PACK):
+                    part = slice(t % 2 * HALF, (t % 2 + 1) * HALF)
+                    nc.vector.scalar_tensor_tensor(
+                        z_rows[:, t * HALF : (t + 1) * HALF],
+                        mx[t // 2][:, part],
+                        gs_t[:, t : t + 1],
+                        sg[t // 2][:, part],
+                        ALU.mult,
+                        ALU.mult,
+                    )
+            z_il = keep.tile([P, PACK * HALF], BF16, name=f"z_il{h}", align_bytes=64)
             nc.scalar.copy(
                 out=z_il[:].rearrange("p (c i t) -> p c t i", i=4, t=PACK),
                 in_=z_rows[:].rearrange("p (t c i) -> p c t i", i=4, t=PACK),
             )
-            z_w = keep.tile([P, n], U32, name=f"z_w{v0}", align_bytes=64)
-            z_s = keep.tile([P, n], U8, name=f"z_s{v0}", align_bytes=64)
+            z_w = keep.tile([P, HALF], U32, name=f"z_w{h}", align_bytes=64)
+            z_s = keep.tile([P, HALF], U8, name=f"z_s{h}", align_bytes=64)
             nc.vector.quantize_mx(out=z_w[:].bitcast(FP8X4), scales=z_s[:], in_=z_il[:])
             for t in range(PACK):
                 acc = psum.tile([P, BANK], F32, name="acc")
                 nc.tensor.matmul_mx(
-                    out=acc[:, :n],
+                    out=acc[:, :HALF],
                     lhsT=xd_w[:, P * t : P * (t + 1)].bitcast(FP8X4),
                     lhsT_scale=xd_s[:, P * t : P * (t + 1)],
                     rhs=z_w[:].bitcast(FP8X4),
@@ -153,36 +172,49 @@ def tile_picked_candpgatekind_none_po_kernel(
                     start=True,
                     stop=True,
                 )
-                nc.scalar.activation(s_t[t][:, v0:v1], acc[:, :n], ACT.Copy, scale=0.0625)
+                nc.scalar.activation(s_t[t][:, v0:v1], acc[:, :HALF], ACT.Copy, scale=0.0625)
+
+        sums = []
+        for h, tags in enumerate((("mx1_1", "z_il1"), ("u1_0", "u1_1"))):
+            u = [keep.tile([P, 2, HALF], F32, name=tags[g], align_bytes=64) for g in range(2)]
             for t in range(PACK):
                 nc.vector.tensor_tensor(
-                    u_all[:, t, v0:v1],
-                    tab_t[t][:].indirect(n2_t[:, v0 // LANES : v1 // LANES]),
-                    s_t[t][:, v0:v1],
+                    u[t // 2][:, t % 2, :],
+                    tab_t[t][:].indirect(n2_t[:, h * HALF // LANES : (h + 1) * HALF // LANES]),
+                    s_t[t][:, h * HALF : (h + 1) * HALF],
                     ALU.add,
                 )
+            sums.append(u)
 
         out_rows = out_0.rearrange("(p t) v -> p t v", t=PACK)
         out_words = out_1[0].rearrange("p c r -> p (c r)").bitcast(I32)
         o_s = keep.tile([P, V], U8, name="o_s", align_bytes=64)
-        for v0, v1 in OUT_CHUNKS:
-            n = v1 - v0
-            paired = keep.tile([P, PACK, n], F32, name=f"paired{v0}")
+        for h, widths in enumerate(((HALF,), (P, P))):
+            paired = [keep.tile([P, 2, HALF], F32, name=f"paired{g}") for g in range(2)]
             for t in range(PACK):
-                nc.vector.tensor_copy(paired[:, t, :], s_t[t][:].indirect(n3_t[:, v0 // LANES : v1 // LANES]))
-            o = keep.tile([P, PACK, n], F32, name=f"o{v0}")
-            nc.vector.tensor_tensor(o[:], u_all[:, :, v0:v1], paired[:], ALU.max)
-            nc.sync.dma_start(out=out_rows[:, :, v0:v1], in_=o[:])
-            o_il = keep.tile([P, PACK * n], BF16, name=f"o_il{v0}", align_bytes=64)
-            dst = o_il[:].rearrange("p (c i t) -> p c t i", i=4, t=PACK)
-            src = o[:].rearrange("p t (c i) -> p c t i", i=4)
-            if v1 == V:
-                nc.vector.tensor_copy(out=dst, in_=src)
-            else:
-                nc.scalar.copy(out=dst, in_=src)
-            o_w = keep.tile([P, n], U32, name=f"o_w{v0}", align_bytes=64)
-            nc.vector.quantize_mx(out=o_w[:].bitcast(FP8X4), scales=o_s[:, v0:v1], in_=o_il[:])
-            nc.sync.dma_start(out=out_words[:, v0:v1], in_=o_w[:].bitcast(I32))
+                nc.vector.tensor_copy(
+                    paired[t // 2][:, t % 2, :], s_t[t][:].indirect(n3_t[:, h * HALF // LANES : (h + 1) * HALF // LANES])
+                )
+            o_w = keep.tile([P, HALF], U32, name=f"o_w{h}", align_bytes=64)
+            c0 = 0
+            for n in widths:
+                v0 = h * HALF + c0
+                o = keep.tile([P, PACK, n], F32, name=f"o{v0}")
+                for g in range(2):
+                    nc.vector.tensor_tensor(
+                        o[:, 2 * g : 2 * g + 2, :], sums[h][g][:, :, c0 : c0 + n], paired[g][:, :, c0 : c0 + n], ALU.max
+                    )
+                nc.sync.dma_start(out=out_rows[:, :, v0 : v0 + n], in_=o[:])
+                o_il = keep.tile([P, PACK * n], BF16, name=f"o_il{v0}", align_bytes=64)
+                dst = o_il[:].rearrange("p (c i t) -> p c t i", i=4, t=PACK)
+                src = o[:].rearrange("p t (c i) -> p c t i", i=4)
+                if v0 + n == V:
+                    nc.vector.tensor_copy(out=dst, in_=src)
+                else:
+                    nc.scalar.copy(out=dst, in_=src)
+                nc.vector.quantize_mx(out=o_w[:, c0 : c0 + n].bitcast(FP8X4), scales=o_s[:, v0 : v0 + n], in_=o_il[:])
+                c0 += n
+            nc.sync.dma_start(out=out_words[:, h * HALF : (h + 1) * HALF], in_=o_w[:].bitcast(I32))
         for q in range(4):
             queue = nc.scalar if q % 2 else nc.sync
             queue.dma_start(out=out_2[0, 4 * q : 4 * q + 4, :].bitcast(I32), in_=o_s[32 * q : 32 * q + 4, :].bitcast(I32))

@@ -55,8 +55,8 @@ def tile_picked_candpgatekind_none_po_kernel(
         nc.sync.dma_start(offs_t[:], offs)
         load_scale_rows(nc.sync, x_s, x_scales[0])
         nc.sync.dma_start(out=x_w[:].bitcast(I32), in_=x_words[0].rearrange("p c r -> p (c r)").bitcast(I32))
-        nc.sync.dma_start(cand_t[:], cand)
         load_scale_rows(nc.sync, ws_raw, w1_scales[0])
+        nc.sync.dma_start(cand_t[:], cand)
         nc.sync.dma_start(n1_t[:], n1)
         nc.sync.dma_start(out=gs_t[:], in_=gs.rearrange("(p t) o -> p (t o)", t=PACK))
         nc.sync.dma_start(n2_t[:], n2)
@@ -74,7 +74,7 @@ def tile_picked_candpgatekind_none_po_kernel(
             out=w_d[:].rearrange("p (t m b) -> p t m b", t=PACK, b=2),
             in_=w_raw[:].rearrange("p (m t b) -> p t m b", t=PACK, b=2),
         )
-        nc.gpsimd.tensor_copy(
+        nc.vector.tensor_copy(
             out=ws_d[:].rearrange("p (t m) -> p t m", t=PACK),
             in_=ws_raw[:].rearrange("p (m t) -> p t m", t=PACK),
         )
@@ -133,26 +133,16 @@ def tile_picked_candpgatekind_none_po_kernel(
             for g in range(2):
                 nc.vector.tensor_tensor(mx[g][:], pairs[g][:, :, 0], pairs[g][:, :, 1], ALU.max)
             z_rows = keep.tile([P, PACK * HALF], BF16, name=f"z_rows{h}", align_bytes=64)
-            if h == 0:
-                for g in range(2):
-                    weighted = keep.tile([P, 2 * HALF], F32, name=f"weighted{g}")
-                    for t in (2 * g, 2 * g + 1):
-                        part = slice(t % 2 * HALF, (t % 2 + 1) * HALF)
-                        nc.scalar.activation(weighted[:, part], mx[g][:, part], ACT.Copy, scale=gs_t[:, t : t + 1])
-                    nc.gpsimd.tensor_tensor(
-                        z_rows[:, 2 * g * HALF : 2 * (g + 1) * HALF], weighted[:], sg[g][:], ALU.mult
-                    )
-            else:
-                for t in range(PACK):
-                    part = slice(t % 2 * HALF, (t % 2 + 1) * HALF)
-                    nc.vector.scalar_tensor_tensor(
-                        z_rows[:, t * HALF : (t + 1) * HALF],
-                        mx[t // 2][:, part],
-                        gs_t[:, t : t + 1],
-                        sg[t // 2][:, part],
-                        ALU.mult,
-                        ALU.mult,
-                    )
+            for t in range(PACK):
+                part = slice(t % 2 * HALF, (t % 2 + 1) * HALF)
+                nc.vector.scalar_tensor_tensor(
+                    z_rows[:, t * HALF : (t + 1) * HALF],
+                    mx[t // 2][:, part],
+                    gs_t[:, t : t + 1],
+                    sg[t // 2][:, part],
+                    ALU.mult,
+                    ALU.mult,
+                )
             z_il = keep.tile([P, PACK * HALF], BF16, name=f"z_il{h}", align_bytes=64)
             nc.scalar.copy(
                 out=z_il[:].rearrange("p (c i t) -> p c t i", i=4, t=PACK),

@@ -13,19 +13,49 @@ FP4X4 = mybir.dt.float4_e2m1fn_x4
 ALU = mybir.AluOpType
 ACT = mybir.ActivationFunctionType
 
-P = 128
-PACK = 4
 K, T, S, V, H, C, J = 512, 2048, 1024, 512, 512, 512, 512
-BANK = 512
-LANES = 16
 FLOPS = 2 * K * H * S + 2 * K * C * V
 
-HALF = 256
+P = 128
+PACK = 4
+QUADRANTS = 4
+BANK = 512
+BANKS = 8
+LANES = 16
+LINE = 4
+HALF = V // 2
+DUO = 2
+
+OUT_BLOCKS = (((0, HALF),), ((0, HALF // 2), (HALF // 2, HALF // 2)))
+
+TAKES_OVER = {
+    "sg0_0": "gate0_2",
+    "mn1_0": "other0_2",
+    "mx1_0": "other0_3",
+    "ln1_1": "ln0_1",
+    "mn1_1": "z_rows0_0",
+    "mx1_1": "z_il0_0",
+    "z_rows1_0": "ln0_1",
+    "sum0_0": "z_rows0_0",
+    "sum0_1": "ln0_1",
+    "paired1_0": "paired0_0",
+    "paired1_1": "paired0_1",
+}
 
 
-def load_scale_rows(queue, tile, rows):
-    for q in range(4):
-        queue.dma_start(out=tile[32 * q : 32 * q + 4, :].bitcast(I32), in_=rows[4 * q : 4 * q + 4, :].bitcast(I32))
+def load_scale_rows(nc, tile, rows):
+    for quad in range(QUADRANTS):
+        nc.sync.dma_start(
+            out=tile[32 * quad : 32 * quad + 4, :].bitcast(I32), in_=rows[4 * quad : 4 * quad + 4, :].bitcast(I32)
+        )
+
+
+def list_slice(tile, first, count):
+    return tile[:, first // LANES : (first + count) // LANES]
+
+
+def duo_tiles(g):
+    return range(DUO * g, DUO * (g + 1))
 
 
 def tile_picked_candpgatekind_none_po_kernel(
@@ -34,7 +64,7 @@ def tile_picked_candpgatekind_none_po_kernel(
     nc = tc.nc
     with ExitStack() as ctx:
         keep = ctx.enter_context(tc.tile_pool(name="keep", bufs=1))
-        psum = ctx.enter_context(tc.psum_pool(name="psum", bufs=8))
+        psum = ctx.enter_context(tc.psum_pool(name="psum", bufs=BANKS))
 
         offs_t = keep.tile([P, S // LANES], U16, name="offs_t")
         cand_t = keep.tile([P, C // LANES], U16, name="cand_t")
@@ -51,11 +81,16 @@ def tile_picked_candpgatekind_none_po_kernel(
         nc.vector.memset(x_s[:].bitcast(I32), 0)
         nc.gpsimd.memset(ws_raw[:].bitcast(I32), 0)
 
+        warm_in = keep.tile([P, 1], F32, name="warm_in")
+        warm_out = keep.tile([P, 1], F32, name="warm_out")
+        nc.gpsimd.memset(warm_in[:], 0.0)
+        nc.scalar.activation(warm_out[:], warm_in[:], ACT.Sigmoid)
+
         nc.sync.dma_start(out=w_raw[:].bitcast(I32), in_=w1_words[0].bitcast(I32))
         nc.sync.dma_start(offs_t[:], offs)
-        load_scale_rows(nc.sync, x_s, x_scales[0])
+        load_scale_rows(nc, x_s, x_scales[0])
         nc.sync.dma_start(out=x_w[:].bitcast(I32), in_=x_words[0].rearrange("p c r -> p (c r)").bitcast(I32))
-        load_scale_rows(nc.sync, ws_raw, w1_scales[0])
+        load_scale_rows(nc, ws_raw, w1_scales[0])
         nc.sync.dma_start(cand_t[:], cand)
         nc.sync.dma_start(n1_t[:], n1)
         nc.sync.dma_start(out=gs_t[:], in_=gs.rearrange("(p t) o -> p (t o)", t=PACK))
@@ -79,20 +114,21 @@ def tile_picked_candpgatekind_none_po_kernel(
             in_=ws_raw[:].rearrange("p (m t) -> p t m", t=PACK),
         )
 
-        xq_w = [keep.tile([P, BANK], U32, name=f"xq_w{h}", align_bytes=64) for h in range(S // BANK)]
-        for h in range(S // BANK):
-            nc.vector.tensor_copy(xq_w[h][:], x_w[:].indirect(offs_t[:, h * BANK // LANES : (h + 1) * BANK // LANES]))
-        y_t = [keep.tile([P, S], F32, name=f"y{t}") for t in range(PACK)]
-        for g in range(2):
-            for h in range(S // BANK):
-                cols = slice(h * BANK, (h + 1) * BANK)
-                for t in (2 * g, 2 * g + 1):
+        stretches = S // BANK
+        xq_w = [keep.tile([P, BANK], U32, name=f"xq_w{c}", align_bytes=64) for c in range(stretches)]
+        for c in range(stretches):
+            nc.vector.tensor_copy(xq_w[c][:], x_w[:].indirect(list_slice(offs_t, c * BANK, BANK)))
+        y_t = [keep.tile([P, S], F32, name=f"y{t}", align_bytes=64) for t in range(PACK)]
+        for g in range(PACK // DUO):
+            for c in range(stretches):
+                cols = slice(c * BANK, (c + 1) * BANK)
+                for t in duo_tiles(g):
                     acc = psum.tile([P, BANK], F32, name="acc")
                     nc.tensor.matmul_mx(
                         out=acc[:],
                         lhsT=w_d[:, 2 * P * t : 2 * P * (t + 1)].bitcast(FP4X4),
                         lhsT_scale=ws_d[:, P * t : P * (t + 1)],
-                        rhs=xq_w[h][:].bitcast(FP8X4),
+                        rhs=xq_w[c][:].bitcast(FP8X4),
                         rhs_scale=xq_s[:, cols],
                         start=True,
                         stop=True,
@@ -110,47 +146,83 @@ def tile_picked_candpgatekind_none_po_kernel(
             in_=xc_s[:].rearrange("p (m t) -> p t m", t=PACK),
         )
         nc.vector.tensor_copy(
-            out=xd_w[:].bitcast(I32).rearrange("p (t m) -> p t m", t=PACK),
-            in_=xc_w[:].bitcast(I32).rearrange("p (m t) -> p t m", t=PACK),
+            out=xd_w[:].bitcast(I32).rearrange("p (t c i) -> p c t i", t=PACK, i=LINE),
+            in_=xc_w[:].bitcast(I32).rearrange("p (c i t) -> p c t i", t=PACK, i=LINE),
         )
 
-        s_t = [keep.tile([P, V], F32, name=f"s{t}") for t in range(PACK)]
-        for h in range(V // HALF):
-            v0, v1 = h * HALF, (h + 1) * HALF
-            ln = [keep.tile([P, 2, 2 * HALF], F32, name=f"ln{(g + h) % 2}", align_bytes=64) for g in range(2)]
-            for t in range(PACK):
-                nc.vector.tensor_copy(
-                    ln[t // 2][:, t % 2, :], y_t[t][:].indirect(n1_t[:, 2 * v0 // LANES : 2 * v1 // LANES])
-                )
-            pairs = [ln[g][:].rearrange("p t (v e) -> p (t v) e", e=2) for g in range(2)]
-            mn = [keep.tile([P, 2 * HALF], F32, name=f"mn{h}_{g}") for g in range(2)]
-            mx_tags = (("mx0_0", "mx0_1"), ("z_il0", "mx1_1"))[h]
-            mx = [keep.tile([P, 2 * HALF], F32, name=mx_tags[g], align_bytes=64) for g in range(2)]
-            sg = [keep.tile([P, 2 * HALF], F32, name=f"sg{h}_{g}") for g in range(2)]
-            for g in range(2):
-                nc.vector.tensor_tensor(mn[g][:], pairs[g][:, :, 0], pairs[g][:, :, 1], ALU.min)
-                nc.scalar.activation(sg[g][:], mn[g][:], ACT.Sigmoid)
-            for g in range(2):
-                nc.vector.tensor_tensor(mx[g][:], pairs[g][:, :, 0], pairs[g][:, :, 1], ALU.max)
-            z_rows = keep.tile([P, PACK * HALF], BF16, name=f"z_rows{h}", align_bytes=64)
-            for t in range(PACK):
-                part = slice(t % 2 * HALF, (t % 2 + 1) * HALF)
+        s_t = [keep.tile([P, V], F32, name=f"s{t}", align_bytes=64) for t in range(PACK)]
+        ln, mx, sg, other, z_rows, z_codes = {}, {}, {}, {}, {}, {}
+
+        def work_tile(kind, h, index, shape, dtype=F32):
+            name = f"{kind}{h}_{index}"
+            return keep.tile(shape, dtype, name=TAKES_OVER.get(name, name), align_bytes=64)
+
+        def lined_up(h, t):
+            return y_t[t][:].indirect(list_slice(n1_t, 2 * h * HALF, 2 * HALF))
+
+        def member(h, g, e):
+            return ln[h, g][:].rearrange("p t (v e) -> p (t v) e", e=2)[:, :, e]
+
+        def z_part(h, t):
+            if h not in z_rows:
+                z_rows[h] = work_tile("z_rows", h, 0, [P, PACK * HALF], BF16)
+            return z_rows[h][:, t * HALF : (t + 1) * HALF]
+
+        def line_up(h, g):
+            ln[h, g] = work_tile("ln", h, g, [P, DUO, 2 * HALF])
+            for t in duo_tiles(g):
+                nc.vector.tensor_copy(ln[h, g][:, t % DUO, :], lined_up(h, t))
+
+        def smaller(h, g):
+            mn = work_tile("mn", h, g, [P, DUO * HALF])
+            sg[h, g] = work_tile("sg", h, g, [P, DUO * HALF])
+            nc.vector.tensor_tensor(mn[:], member(h, g, 0), member(h, g, 1), ALU.min)
+            nc.scalar.activation(sg[h, g][:], mn[:], ACT.Sigmoid)
+
+        def larger(h, g):
+            mx[h, g] = work_tile("mx", h, g, [P, DUO * HALF])
+            nc.vector.tensor_tensor(mx[h, g][:], member(h, g, 0), member(h, g, 1), ALU.max)
+
+        def gate_and_weigh(h, g):
+            for t in duo_tiles(g):
+                part = slice(t % DUO * HALF, (t % DUO + 1) * HALF)
                 nc.vector.scalar_tensor_tensor(
-                    z_rows[:, t * HALF : (t + 1) * HALF],
-                    mx[t // 2][:, part],
-                    gs_t[:, t : t + 1],
-                    sg[t // 2][:, part],
-                    ALU.mult,
-                    ALU.mult,
+                    z_part(h, t), mx[h, g][:, part], gs_t[:, t : t + 1], sg[h, g][:, part], ALU.mult, ALU.mult
                 )
-            z_il = keep.tile([P, PACK * HALF], BF16, name=f"z_il{h}", align_bytes=64)
+
+        def neighbours_gates(h, g):
+            for t in duo_tiles(g):
+                gate = work_tile("gate", h, t, [P, 2 * HALF])
+                nc.scalar.activation(gate[:], lined_up(h, t), ACT.Sigmoid)
+                other[h, t] = work_tile("other", h, t, [P, 2 * HALF])
+                nc.scalar.copy(
+                    out=other[h, t][:].rearrange("p (v e) -> p v e", e=2),
+                    in_=gate[:].rearrange("p (v e) -> p v e", e=2)[:, :, ::-1],
+                )
+
+        def line_up_gated(h, g):
+            ln[h, g] = work_tile("ln", h, g, [P, DUO, 2 * HALF])
+            for t in duo_tiles(g):
+                nc.vector.tensor_tensor(ln[h, g][:, t % DUO, :], lined_up(h, t), other[h, t][:], ALU.mult)
+
+        def weigh(h, g):
+            for t in duo_tiles(g):
+                part = slice(t % DUO * HALF, (t % DUO + 1) * HALF)
+                nc.scalar.activation(z_part(h, t), mx[h, g][:, part], ACT.Copy, scale=gs_t[:, t : t + 1])
+
+        def quantise(h):
+            z_il = work_tile("z_il", h, 0, [P, PACK * HALF], BF16)
             nc.scalar.copy(
-                out=z_il[:].rearrange("p (c i t) -> p c t i", i=4, t=PACK),
-                in_=z_rows[:].rearrange("p (t c i) -> p c t i", i=4, t=PACK),
+                out=z_il[:].rearrange("p (c i t) -> p c t i", i=LINE, t=PACK),
+                in_=z_rows[h][:].rearrange("p (t c i) -> p c t i", i=LINE, t=PACK),
             )
             z_w = keep.tile([P, HALF], U32, name=f"z_w{h}", align_bytes=64)
             z_s = keep.tile([P, HALF], U8, name=f"z_s{h}", align_bytes=64)
             nc.vector.quantize_mx(out=z_w[:].bitcast(FP8X4), scales=z_s[:], in_=z_il[:])
+            z_codes[h] = (z_w, z_s)
+
+        def score(h):
+            z_w, z_s = z_codes[h]
             for t in range(PACK):
                 acc = psum.tile([P, BANK], F32, name="acc")
                 nc.tensor.matmul_mx(
@@ -162,49 +234,74 @@ def tile_picked_candpgatekind_none_po_kernel(
                     start=True,
                     stop=True,
                 )
-                nc.scalar.activation(s_t[t][:, v0:v1], acc[:, :HALF], ACT.Copy, scale=0.0625)
+                nc.scalar.activation(s_t[t][:, h * HALF : (h + 1) * HALF], acc[:, :HALF], ACT.Copy, scale=0.0625)
 
-        sums = []
-        for h, tags in enumerate((("mx1_1", "z_il1"), ("u1_0", "u1_1"))):
-            u = [keep.tile([P, 2, HALF], F32, name=tags[g], align_bytes=64) for g in range(2)]
-            for t in range(PACK):
-                nc.vector.tensor_tensor(
-                    u[t // 2][:, t % 2, :],
-                    tab_t[t][:].indirect(n2_t[:, h * HALF // LANES : (h + 1) * HALF // LANES]),
-                    s_t[t][:, h * HALF : (h + 1) * HALF],
-                    ALU.add,
-                )
-            sums.append(u)
+        line_up(0, 0)
+        line_up(1, 0)
+        neighbours_gates(0, 1)
+        smaller(0, 0)
+        larger(0, 0)
+        gate_and_weigh(0, 0)
+        line_up_gated(0, 1)
+        smaller(1, 0)
+        larger(0, 1)
+        weigh(0, 1)
+        larger(1, 0)
+        line_up(1, 1)
+        quantise(0)
+        smaller(1, 1)
+        score(0)
+        larger(1, 1)
+        gate_and_weigh(1, 0)
+        gate_and_weigh(1, 1)
+        quantise(1)
+        score(1)
+
+        sums = {}
+        for h in range(V // HALF):
+            for g in range(PACK // DUO):
+                sums[h, g] = work_tile("sum", h, g, [P, DUO, HALF])
+                for t in duo_tiles(g):
+                    nc.vector.tensor_tensor(
+                        sums[h, g][:, t % DUO, :],
+                        tab_t[t][:].indirect(list_slice(n2_t, h * HALF, HALF)),
+                        s_t[t][:, h * HALF : (h + 1) * HALF],
+                        ALU.add,
+                    )
 
         out_rows = out_0.rearrange("(p t) v -> p t v", t=PACK)
         out_words = out_1[0].rearrange("p c r -> p (c r)").bitcast(I32)
         o_s = keep.tile([P, V], U8, name="o_s", align_bytes=64)
-        for h, widths in enumerate(((HALF,), (P, P))):
-            paired = [keep.tile([P, 2, HALF], F32, name=f"paired{g}") for g in range(2)]
+        for h in range(V // HALF):
+            paired = [work_tile("paired", h, g, [P, DUO, HALF]) for g in range(PACK // DUO)]
             for t in range(PACK):
                 nc.vector.tensor_copy(
-                    paired[t // 2][:, t % 2, :], s_t[t][:].indirect(n3_t[:, h * HALF // LANES : (h + 1) * HALF // LANES])
+                    paired[t // DUO][:, t % DUO, :], s_t[t][:].indirect(list_slice(n3_t, h * HALF, HALF))
                 )
             o_w = keep.tile([P, HALF], U32, name=f"o_w{h}", align_bytes=64)
-            c0 = 0
-            for n in widths:
+            for b, (c0, n) in enumerate(OUT_BLOCKS[h]):
                 v0 = h * HALF + c0
-                o = keep.tile([P, PACK, n], F32, name=f"o{v0}")
-                for g in range(2):
+                o = work_tile("o", h, b, [P, PACK, n])
+                for g in range(PACK // DUO):
                     nc.vector.tensor_tensor(
-                        o[:, 2 * g : 2 * g + 2, :], sums[h][g][:, :, c0 : c0 + n], paired[g][:, :, c0 : c0 + n], ALU.max
+                        o[:, DUO * g : DUO * (g + 1), :],
+                        sums[h, g][:, :, c0 : c0 + n],
+                        paired[g][:, :, c0 : c0 + n],
+                        ALU.max,
                     )
                 nc.sync.dma_start(out=out_rows[:, :, v0 : v0 + n], in_=o[:])
-                o_il = keep.tile([P, PACK * n], BF16, name=f"o_il{v0}", align_bytes=64)
-                dst = o_il[:].rearrange("p (c i t) -> p c t i", i=4, t=PACK)
-                src = o[:].rearrange("p t (c i) -> p c t i", i=4)
+                o_il = work_tile("o_il", h, b, [P, PACK * n], BF16)
+                dst = o_il[:].rearrange("p (c i t) -> p c t i", i=LINE, t=PACK)
+                src = o[:].rearrange("p t (c i) -> p c t i", i=LINE)
                 if v0 + n == V:
                     nc.vector.tensor_copy(out=dst, in_=src)
                 else:
                     nc.scalar.copy(out=dst, in_=src)
                 nc.vector.quantize_mx(out=o_w[:, c0 : c0 + n].bitcast(FP8X4), scales=o_s[:, v0 : v0 + n], in_=o_il[:])
-                c0 += n
             nc.sync.dma_start(out=out_words[:, h * HALF : (h + 1) * HALF], in_=o_w[:].bitcast(I32))
-        for q in range(4):
-            queue = nc.scalar if q % 2 else nc.sync
-            queue.dma_start(out=out_2[0, 4 * q : 4 * q + 4, :].bitcast(I32), in_=o_s[32 * q : 32 * q + 4, :].bitcast(I32))
+        for quad in range(QUADRANTS):
+            queue = nc.scalar if quad % 2 else nc.sync
+            queue.dma_start(
+                out=out_2[0, 4 * quad : 4 * quad + 4, :].bitcast(I32),
+                in_=o_s[32 * quad : 32 * quad + 4, :].bitcast(I32),
+            )

from contextlib import ExitStack

import concourse.mybir as mybir

F32 = mybir.dt.float32
BF16 = mybir.dt.bfloat16
I32 = mybir.dt.int32
U32 = mybir.dt.uint32
U16 = mybir.dt.uint16
U8 = mybir.dt.uint8
FP8X4 = mybir.dt.float8_e4m3fn_x4
FP4X4 = mybir.dt.float4_e2m1fn_x4
ALU = mybir.AluOpType
ACT = mybir.ActivationFunctionType

K, T, S, V, H, C, J = 512, 2048, 1024, 512, 512, 512, 512
FLOPS = 2 * K * H * S + 2 * K * C * V

P = 128
PACK = 4
QUADRANTS = 4
BANK = 512
BANKS = 8
LANES = 16
LINE = 4
HALF = V // 2
DUO = 2

OUT_BLOCKS = (((0, HALF),), ((0, HALF // 2), (HALF // 2, HALF // 2)))

TAKES_OVER = {
    "sg0_0": "gate0_2",
    "mn1_0": "other0_2",
    "mx1_0": "other0_3",
    "ln1_1": "ln0_1",
    "mn1_1": "z_rows0_0",
    "mx1_1": "z_il0_0",
    "z_rows1_0": "ln0_1",
    "sum0_0": "z_rows0_0",
    "sum0_1": "ln0_1",
    "paired1_0": "paired0_0",
    "paired1_1": "paired0_1",
}


def load_scale_rows(nc, tile, rows):
    for quad in range(QUADRANTS):
        nc.sync.dma_start(
            out=tile[32 * quad : 32 * quad + 4, :].bitcast(I32), in_=rows[4 * quad : 4 * quad + 4, :].bitcast(I32)
        )


def list_slice(tile, first, count):
    return tile[:, first // LANES : (first + count) // LANES]


def duo_tiles(g):
    return range(DUO * g, DUO * (g + 1))


def tile_picked_candpgatekind_none_po_kernel(
    tc, x_words, x_scales, w1_words, w1_scales, gs, tab, offs, n1, cand, n2, n3, out_0, out_1, out_2
):
    nc = tc.nc
    with ExitStack() as ctx:
        keep = ctx.enter_context(tc.tile_pool(name="keep", bufs=1))
        psum = ctx.enter_context(tc.psum_pool(name="psum", bufs=BANKS))

        offs_t = keep.tile([P, S // LANES], U16, name="offs_t")
        cand_t = keep.tile([P, C // LANES], U16, name="cand_t")
        n1_t = keep.tile([P, S // LANES], U16, name="n1_t")
        n2_t = keep.tile([P, V // LANES], U16, name="n2_t")
        n3_t = keep.tile([P, V // LANES], U16, name="n3_t")
        x_w = keep.tile([P, T], U32, name="x_w", align_bytes=64)
        x_s = keep.tile([P, T], U8, name="x_s", align_bytes=64)
        w_raw = keep.tile([P, 2 * H], U8, name="w_raw", align_bytes=64)
        ws_raw = keep.tile([P, H], U8, name="ws_raw", align_bytes=64)
        gs_t = keep.tile([P, PACK], F32, name="gs_t")
        tab_t = [keep.tile([P, J], F32, name=f"tab{t}") for t in range(PACK)]

        nc.vector.memset(x_s[:].bitcast(I32), 0)
        nc.gpsimd.memset(ws_raw[:].bitcast(I32), 0)

        warm_in = keep.tile([P, 1], F32, name="warm_in")
        warm_out = keep.tile([P, 1], F32, name="warm_out")
        nc.gpsimd.memset(warm_in[:], 0.0)
        nc.scalar.activation(warm_out[:], warm_in[:], ACT.Sigmoid)

        nc.sync.dma_start(out=w_raw[:].bitcast(I32), in_=w1_words[0].bitcast(I32))
        nc.sync.dma_start(offs_t[:], offs)
        load_scale_rows(nc, x_s, x_scales[0])
        nc.sync.dma_start(out=x_w[:].bitcast(I32), in_=x_words[0].rearrange("p c r -> p (c r)").bitcast(I32))
        load_scale_rows(nc, ws_raw, w1_scales[0])
        nc.sync.dma_start(cand_t[:], cand)
        nc.sync.dma_start(n1_t[:], n1)
        nc.sync.dma_start(out=gs_t[:], in_=gs.rearrange("(p t) o -> p (t o)", t=PACK))
        nc.sync.dma_start(n2_t[:], n2)
        nc.sync.dma_start(n3_t[:], n3)
        tab_rows = tab.rearrange("(p t) j -> p t j", t=PACK)
        for t in range(PACK):
            nc.sync.dma_start(out=tab_t[t][:], in_=tab_rows[:, t, :])

        xq_s = keep.tile([P, S], U8, name="xq_s", align_bytes=64)
        nc.vector.tensor_copy(xq_s[:], x_s[:].indirect(offs_t[:]))

        w_d = keep.tile([P, 2 * H], U8, name="w_d", align_bytes=64)
        ws_d = keep.tile([P, H], U8, name="ws_d", align_bytes=64)
        nc.vector.tensor_copy(
            out=w_d[:].rearrange("p (t m b) -> p t m b", t=PACK, b=2),
            in_=w_raw[:].rearrange("p (m t b) -> p t m b", t=PACK, b=2),
        )
        nc.vector.tensor_copy(
            out=ws_d[:].rearrange("p (t m) -> p t m", t=PACK),
            in_=ws_raw[:].rearrange("p (m t) -> p t m", t=PACK),
        )

        stretches = S // BANK
        xq_w = [keep.tile([P, BANK], U32, name=f"xq_w{c}", align_bytes=64) for c in range(stretches)]
        for c in range(stretches):
            nc.vector.tensor_copy(xq_w[c][:], x_w[:].indirect(list_slice(offs_t, c * BANK, BANK)))
        y_t = [keep.tile([P, S], F32, name=f"y{t}", align_bytes=64) for t in range(PACK)]
        for g in range(PACK // DUO):
            for c in range(stretches):
                cols = slice(c * BANK, (c + 1) * BANK)
                for t in duo_tiles(g):
                    acc = psum.tile([P, BANK], F32, name="acc")
                    nc.tensor.matmul_mx(
                        out=acc[:],
                        lhsT=w_d[:, 2 * P * t : 2 * P * (t + 1)].bitcast(FP4X4),
                        lhsT_scale=ws_d[:, P * t : P * (t + 1)],
                        rhs=xq_w[c][:].bitcast(FP8X4),
                        rhs_scale=xq_s[:, cols],
                        start=True,
                        stop=True,
                    )
                    nc.scalar.copy(out=y_t[t][:, cols], in_=acc[:])

        xc_s = keep.tile([P, C], U8, name="xc_s", align_bytes=64)
        xc_w = keep.tile([P, C], U32, name="xc_w", align_bytes=64)
        xd_s = keep.tile([P, C], U8, name="xd_s", align_bytes=64)
        xd_w = keep.tile([P, C], U32, name="xd_w", align_bytes=64)
        nc.vector.tensor_copy(xc_s[:], x_s[:].indirect(cand_t[:]))
        nc.vector.tensor_copy(xc_w[:], x_w[:].indirect(cand_t[:]))
        nc.vector.tensor_copy(
            out=xd_s[:].rearrange("p (t m) -> p t m", t=PACK),
            in_=xc_s[:].rearrange("p (m t) -> p t m", t=PACK),
        )
        nc.vector.tensor_copy(
            out=xd_w[:].bitcast(I32).rearrange("p (t c i) -> p c t i", t=PACK, i=LINE),
            in_=xc_w[:].bitcast(I32).rearrange("p (c i t) -> p c t i", t=PACK, i=LINE),
        )

        s_t = [keep.tile([P, V], F32, name=f"s{t}", align_bytes=64) for t in range(PACK)]
        ln, mx, sg, other, z_rows, z_codes = {}, {}, {}, {}, {}, {}

        def work_tile(kind, h, index, shape, dtype=F32):
            name = f"{kind}{h}_{index}"
            return keep.tile(shape, dtype, name=TAKES_OVER.get(name, name), align_bytes=64)

        def lined_up(h, t):
            return y_t[t][:].indirect(list_slice(n1_t, 2 * h * HALF, 2 * HALF))

        def member(h, g, e):
            return ln[h, g][:].rearrange("p t (v e) -> p (t v) e", e=2)[:, :, e]

        def z_part(h, t):
            if h not in z_rows:
                z_rows[h] = work_tile("z_rows", h, 0, [P, PACK * HALF], BF16)
            return z_rows[h][:, t * HALF : (t + 1) * HALF]

        def line_up(h, g):
            ln[h, g] = work_tile("ln", h, g, [P, DUO, 2 * HALF])
            for t in duo_tiles(g):
                nc.vector.tensor_copy(ln[h, g][:, t % DUO, :], lined_up(h, t))

        def smaller(h, g):
            mn = work_tile("mn", h, g, [P, DUO * HALF])
            sg[h, g] = work_tile("sg", h, g, [P, DUO * HALF])
            nc.vector.tensor_tensor(mn[:], member(h, g, 0), member(h, g, 1), ALU.min)
            nc.scalar.activation(sg[h, g][:], mn[:], ACT.Sigmoid)

        def larger(h, g):
            mx[h, g] = work_tile("mx", h, g, [P, DUO * HALF])
            nc.vector.tensor_tensor(mx[h, g][:], member(h, g, 0), member(h, g, 1), ALU.max)

        def gate_and_weigh(h, g):
            for t in duo_tiles(g):
                part = slice(t % DUO * HALF, (t % DUO + 1) * HALF)
                nc.vector.scalar_tensor_tensor(
                    z_part(h, t), mx[h, g][:, part], gs_t[:, t : t + 1], sg[h, g][:, part], ALU.mult, ALU.mult
                )

        def neighbours_gates(h, g):
            for t in duo_tiles(g):
                gate = work_tile("gate", h, t, [P, 2 * HALF])
                nc.scalar.activation(gate[:], lined_up(h, t), ACT.Sigmoid)
                other[h, t] = work_tile("other", h, t, [P, 2 * HALF])
                nc.scalar.copy(
                    out=other[h, t][:].rearrange("p (v e) -> p v e", e=2),
                    in_=gate[:].rearrange("p (v e) -> p v e", e=2)[:, :, ::-1],
                )

        def line_up_gated(h, g):
            ln[h, g] = work_tile("ln", h, g, [P, DUO, 2 * HALF])
            for t in duo_tiles(g):
                nc.vector.tensor_tensor(ln[h, g][:, t % DUO, :], lined_up(h, t), other[h, t][:], ALU.mult)

        def weigh(h, g):
            for t in duo_tiles(g):
                part = slice(t % DUO * HALF, (t % DUO + 1) * HALF)
                nc.scalar.activation(z_part(h, t), mx[h, g][:, part], ACT.Copy, scale=gs_t[:, t : t + 1])

        def quantise(h):
            z_il = work_tile("z_il", h, 0, [P, PACK * HALF], BF16)
            nc.scalar.copy(
                out=z_il[:].rearrange("p (c i t) -> p c t i", i=LINE, t=PACK),
                in_=z_rows[h][:].rearrange("p (t c i) -> p c t i", i=LINE, t=PACK),
            )
            z_w = keep.tile([P, HALF], U32, name=f"z_w{h}", align_bytes=64)
            z_s = keep.tile([P, HALF], U8, name=f"z_s{h}", align_bytes=64)
            nc.vector.quantize_mx(out=z_w[:].bitcast(FP8X4), scales=z_s[:], in_=z_il[:])
            z_codes[h] = (z_w, z_s)

        def score(h):
            z_w, z_s = z_codes[h]
            for t in range(PACK):
                acc = psum.tile([P, BANK], F32, name="acc")
                nc.tensor.matmul_mx(
                    out=acc[:, :HALF],
                    lhsT=xd_w[:, P * t : P * (t + 1)].bitcast(FP8X4),
                    lhsT_scale=xd_s[:, P * t : P * (t + 1)],
                    rhs=z_w[:].bitcast(FP8X4),
                    rhs_scale=z_s[:],
                    start=True,
                    stop=True,
                )
                nc.scalar.activation(s_t[t][:, h * HALF : (h + 1) * HALF], acc[:, :HALF], ACT.Copy, scale=0.0625)

        line_up(0, 0)
        line_up(1, 0)
        neighbours_gates(0, 1)
        smaller(0, 0)
        larger(0, 0)
        gate_and_weigh(0, 0)
        line_up_gated(0, 1)
        smaller(1, 0)
        larger(0, 1)
        weigh(0, 1)
        larger(1, 0)
        line_up(1, 1)
        quantise(0)
        smaller(1, 1)
        score(0)
        larger(1, 1)
        gate_and_weigh(1, 0)
        gate_and_weigh(1, 1)
        quantise(1)
        score(1)

        sums = {}
        for h in range(V // HALF):
            for g in range(PACK // DUO):
                sums[h, g] = work_tile("sum", h, g, [P, DUO, HALF])
                for t in duo_tiles(g):
                    nc.vector.tensor_tensor(
                        sums[h, g][:, t % DUO, :],
                        tab_t[t][:].indirect(list_slice(n2_t, h * HALF, HALF)),
                        s_t[t][:, h * HALF : (h + 1) * HALF],
                        ALU.add,
                    )

        out_rows = out_0.rearrange("(p t) v -> p t v", t=PACK)
        out_words = out_1[0].rearrange("p c r -> p (c r)").bitcast(I32)
        o_s = keep.tile([P, V], U8, name="o_s", align_bytes=64)
        for h in range(V // HALF):
            paired = [work_tile("paired", h, g, [P, DUO, HALF]) for g in range(PACK // DUO)]
            for t in range(PACK):
                nc.vector.tensor_copy(
                    paired[t // DUO][:, t % DUO, :], s_t[t][:].indirect(list_slice(n3_t, h * HALF, HALF))
                )
            o_w = keep.tile([P, HALF], U32, name=f"o_w{h}", align_bytes=64)
            for b, (c0, n) in enumerate(OUT_BLOCKS[h]):
                v0 = h * HALF + c0
                o = work_tile("o", h, b, [P, PACK, n])
                for g in range(PACK // DUO):
                    nc.vector.tensor_tensor(
                        o[:, DUO * g : DUO * (g + 1), :],
                        sums[h, g][:, :, c0 : c0 + n],
                        paired[g][:, :, c0 : c0 + n],
                        ALU.max,
                    )
                nc.sync.dma_start(out=out_rows[:, :, v0 : v0 + n], in_=o[:])
                o_il = work_tile("o_il", h, b, [P, PACK * n], BF16)
                dst = o_il[:].rearrange("p (c i t) -> p c t i", i=LINE, t=PACK)
                src = o[:].rearrange("p t (c i) -> p c t i", i=LINE)
                if v0 + n == V:
                    nc.vector.tensor_copy(out=dst, in_=src)
                else:
                    nc.scalar.copy(out=dst, in_=src)
                nc.vector.quantize_mx(out=o_w[:, c0 : c0 + n].bitcast(FP8X4), scales=o_s[:, v0 : v0 + n], in_=o_il[:])
            nc.sync.dma_start(out=out_words[:, h * HALF : (h + 1) * HALF], in_=o_w[:].bitcast(I32))
        for quad in range(QUADRANTS):
            queue = nc.scalar if quad % 2 else nc.sync
            queue.dma_start(
                out=out_2[0, 4 * quad : 4 * quad + 4, :].bitcast(I32),
                in_=o_s[32 * quad : 32 * quad + 4, :].bitcast(I32),
            )
